import numpy as np
import ml_dtypes


def mxq(x, axis, fmt="e4m3"):
    dtype, down = {"e4m3": (ml_dtypes.float8_e4m3fn, 7), "e5m2": (ml_dtypes.float8_e5m2, 14)}[fmt]
    v = np.moveaxis(np.asarray(x, np.float32).astype(ml_dtypes.bfloat16).astype(np.float64), axis, -1)
    blocks = v.reshape(v.shape[:-1] + (-1, 32))
    amax = np.abs(blocks).max(-1, keepdims=True)
    byte = np.maximum(np.where(amax > 0, np.frexp(amax)[1] - 1 + 127, 0) - down, 1)
    scale = np.exp2(byte - 127.0)
    codes = (blocks / scale).astype(np.float32).astype(dtype).astype(np.float64)
    return np.moveaxis((codes * scale).reshape(v.shape), -1, axis)


WIDE = False


def mx_kscale(k):
    if not WIDE:
        return np.ones(k)
    levels = np.array([30, -30])
    if k % 512:
        return np.exp2(np.random.permutation(np.resize(levels, k // 32))).repeat(32)
    a = np.empty((k // 512, 16))
    for p in range(k // 512):
        a[p, :8] = np.random.permutation(np.resize(levels, 8))
        for g in range(8):
            far = levels[np.abs(levels - a[p, g]) >= 10]
            a[p, g + 8] = far[np.random.randint(len(far))]
    return np.exp2(a.ravel()).repeat(32)


BF16 = ml_dtypes.bfloat16


def bf(x):
    return np.asarray(x, np.float32).astype(BF16)


def f64(x):
    return np.asarray(x).astype(np.float64)


A, B, F, C = 1024, 2048, 1536, 512

E2M1 = np.array([0, 0.5, 1, 1.5, 2, 3, 4, 6, -0.0, -0.5, -1, -1.5, -2, -3, -4, -6])


def setup_inputs():
    s, t, r = mx_kscale(B), mx_kscale(F), mx_kscale(A)
    ds = np.random.standard_normal((A, B)) * np.exp(0.5 * np.random.standard_normal((A, B)))
    z = np.random.standard_normal((B, F)) / np.sqrt(B)
    row = (1 + 0.1 * np.random.standard_normal((C, 1))) / (3 * np.sqrt(F))
    metric = np.random.choice(E2M1, (C, F)) * row
    return {"ds": bf(ds * s * r[:, None]),
            "z": bf(z / s[:, None]),
            "d": bf(np.random.uniform(0.2, 1.1, (A, F))),
            "g": bf((1 + 0.1 * np.random.standard_normal(F)) * t),
            "metric": bf(metric / t),
            "x": bf(np.random.standard_normal((A, C)) / np.sqrt(A) / r[:, None])}


def reference(ds, z, d, g, metric, x):
    du = mxq(f64(ds), 1, "e5m2") @ mxq(f64(z), 0, "e4m3")
    dp = du * f64(g) * f64(d)
    dx = mxq(dp, 1, "e5m2") @ mxq(f64(metric), 1, "e4m3").T
    dmetric = mxq(f64(x), 0, "e4m3").T @ mxq(dp, 0, "e5m2")
    return dx, dmetric

@@ -1,0 +1,351 @@
+from contextlib import ExitStack
+
+import concourse.mybir as mybir
+from concourse.masks import make_identity
+
+A, B, F, C = 1024, 2048, 1536, 512
+FLOPS = 2 * A * B * F + 4 * A * F * C
+
+F32 = mybir.dt.float32
+BF16 = mybir.dt.bfloat16
+U32 = mybir.dt.uint32
+U8 = mybir.dt.uint8
+E4M3 = mybir.dt.float8_e4m3fn_x4
+E5M2 = mybir.dt.float8_e5m2_x4
+MULT = mybir.AluOpType.mult
+
+P = 128
+W = 512
+
+
+def tile_pair_score_metric_backward_s6_kernel(tc, ds, z, d, g, metric, x, out_0, out_1):
+    nc = tc.nc
+    with ExitStack() as ctx:
+        sb = ctx.enter_context(tc.tile_pool(name="sb", bufs=1))
+        ps = ctx.enter_context(tc.psum_pool(name="ps", bufs=1))
+        ctx.enter_context(tc.manual_schedule())
+
+        def tiles(name, count, width, dtype):
+            return [sb.tile([P, width], dtype, name="%s%d" % (name, i), align_bytes=64) for i in range(count)]
+
+        def operands(name, count):
+            return list(zip(tiles(name + "c", count, W, U32), tiles(name + "s", count, W, U8)))
+
+        free = {
+            "bank": [ps.tile([P, W], F32, name="bank%d" % i) for i in range(8)],
+            "raw": tiles("raw", 16, 4 * W, BF16),
+            "grp": tiles("grp", 7, 4 * W, BF16),
+            "gd": tiles("gd", 4, W, F32),
+            "dp": tiles("dp", 6, 4 * W, BF16),
+            "res": tiles("res", 8, W, F32),
+            "e4": operands("e4", 13),
+            "e5": operands("e5", 18),
+        }
+        ident = tiles("ident", 1, P, F32)[0]
+        g_words = tiles("gw", 1, 6, F32)[0]
+        g_all = tiles("gall", 1, F, BF16)[0]
+        make_identity(nc, ident[:])
+
+        have = {}
+        done = set()
+        left = {}
+
+        def take(kind, key, uses):
+            have[key] = free[kind].pop(0)
+            left[key] = [kind, uses]
+            return have[key]
+
+        def used(key, amount=1):
+            left[key][1] -= amount
+            if left[key][1] == 0:
+                kind = left.pop(key)[0]
+                free[kind].append(have.pop(key))
+                if kind == "raw":
+                    load_more()
+
+        def rows4(src):
+            return src.rearrange("(p j) w -> p j w", j=4)
+
+        def blk(i):
+            return slice(i * W, (i + 1) * W)
+
+        def source(key):
+            if key[0] == "x":
+                return rows4(x[blk(key[1]), :]), W
+            if key[0] == "ds":
+                return rows4(ds[blk(key[1]), :])[:, key[2], :].rearrange("p (j w) -> p j w", j=4), 2
+            if key[0] == "d":
+                return rows4(d[blk(key[1]), blk(key[2])]), 4
+            if key[0] == "m":
+                return metric[:, blk(key[1])].rearrange("(j p) w -> p j w", j=4), 2
+            return rows4(z[blk(key[2]), blk(key[1])]), W
+
+        order = [key for k in range(4) for key in (("z", 0, k), ("ds", 0, k))] + [("z", 1, 0), ("d", 0, 0), ("ds", 1, 0), ("ds", 1, 1), ("z", 1, 1), ("d", 1, 0), ("ds", 1, 2), ("ds", 1, 3), ("z", 1, 2), ("z", 1, 3), ("d", 0, 1), ("z", 2, 0), ("d", 1, 1)] + [("z", 2, k) for k in range(1, 4)] + [("d", 0, 2)] + [("m", q) for q in range(3)] + [("d", 1, 2), ("x", 0), ("x", 1)]
+
+        def load_more():
+            while order and free["raw"]:
+                key = order.pop(0)
+                src, uses = source(key)
+                tile = take("raw", ("in",) + key, uses)
+                nc.sync.dma_start(out=tile[:].rearrange("p (j w) -> p j w", j=4), in_=src)
+                done.add(("in",) + key)
+                if key == ("ds", 0, 0):
+                    nc.sync.dma_start(
+                        out=g_words[:].rearrange("p (a c) -> p a c", a=2),
+                        in_=g.bitcast(F32).rearrange("(a p c) -> p a c", a=2, c=3),
+                    )
+
+        def copy(eng, out, in_):
+            if eng == "V":
+                nc.vector.tensor_copy(out=out, in_=in_)
+            else:
+                nc.scalar.copy(out=out, in_=in_)
+
+        def obtain(kind, key, uses):
+            if key not in have:
+                if not free[kind]:
+                    return None
+                take(kind, key, uses)
+            return have[key]
+
+        def filled(key, amount, total):
+            left["fill", key] = left.get(("fill", key), 0) + amount
+            if left["fill", key] == total:
+                done.add(key)
+
+        def weave(eng, key, lo, hi):
+            src = ("in",) + key[1:] if key[0] == "w" else ("in",) + key
+            if src not in done:
+                return False
+            dst = obtain("grp", ("grp",) + key, 1)
+            if dst is None:
+                return False
+            rows = have[src][:].rearrange("p (t c i) -> p c t i", t=4, i=4)
+            side = dst[:].rearrange("p (c i t) -> p c t i", t=4, i=4)
+            copy(eng, side[:, lo // 4 : hi // 4], rows[:, lo // 4 : hi // 4])
+            used(src, hi - lo)
+            filled(("grp",) + key, hi - lo, W)
+            return True
+
+        uses_of = {"z": 8, "ds": 12, "m": 8, "x": 12, "dp": 4, "w": 4}
+
+        def quant(eng, key):
+            kind = "e4" if key[0] in ("z", "m", "x") else "e5"
+            if ("grp",) + key not in done or not free[kind]:
+                return False
+            operand = take(kind, ("q",) + key, uses_of[key[0]])
+            nc.vector.quantize_mx(
+                out=operand[0][:].bitcast(E4M3 if kind == "e4" else E5M2), scales=operand[1][:], in_=have[("grp",) + key][:]
+            )
+            used(("grp",) + key)
+            done.add(("q",) + key)
+            return True
+
+        def turn(eng, key, half):
+            src = ("in",) + key
+            need = ("part", half) + key if key[0] == "dp" else src
+            if need not in done or not free["bank"]:
+                return False
+            bank = take("bank", ("t", half) + key, 1)
+            words = have[src][:].bitcast(F32)
+            for j in range(2):
+                first = 256 * (2 * half + j)
+                for u in range(2):
+                    if key[0] == "dp":
+                        part = words[:, first + P * u : first + P * (u + 1)]
+                    else:
+                        part = words[:, first + u : first + 256 : 2]
+                    nc.tensor.transpose(bank[:, (2 * j + u) * P : (2 * j + u + 1) * P], part, ident[:])
+            used(src)
+            done.add(("t", half) + key)
+            return True
+
+        def pairs(eng, key, half):
+            if ("t", half) + key not in done:
+                return False
+            dst = obtain("grp", ("grp",) + key, 1)
+            if dst is None:
+                return False
+            copy(
+                eng,
+                dst[:].bitcast(F32)[:, blk(half)].rearrange("p (j r u) -> p j r u", j=2, u=2),
+                have[("t", half) + key][:].rearrange("p (j u r) -> p j r u", j=2, u=2),
+            )
+            used(("t", half) + key)
+            filled(("grp",) + key, 1, 2)
+            return True
+
+        def mm(acc, still, col, moving, step, steps):
+            if ("q",) + still not in done or ("q",) + moving not in done:
+                return False
+            bank = obtain("bank", acc, 1)
+            if bank is None:
+                return False
+            cols = slice(col * P, (col + 1) * P)
+            a, b = have[("q",) + still], have[("q",) + moving]
+            nc.tensor.matmul_mx(
+                out=bank[:],
+                lhsT=a[0][:, cols].bitcast(E4M3 if still[0] == "x" else E5M2),
+                lhsT_scale=a[1][:, cols],
+                rhs=b[0][:].bitcast(E5M2 if still[0] == "x" else E4M3),
+                rhs_scale=b[1][:],
+                start=step == 0,
+                stop=step == steps - 1,
+            )
+            used(("q",) + still)
+            used(("q",) + moving)
+            filled(acc, 1, steps)
+            return True
+
+        def du(eng, h, q, t, k):
+            return mm(("du", h, q, t), ("ds", h, t), k, ("z", q, k), k, 4)
+
+        def dm(eng, q, c, h):
+            return mm(("dm", q, c), ("x", h), c, ("w", "dp", h, q), h, 2)
+
+        def dx(eng, h, t, q):
+            return mm(("dx", h, t), ("dp", h, q), t, ("m", q), q, 3)
+
+        def spread(eng, part):
+            if not free["bank"]:
+                return False
+            bank = take("bank", ("g", part), 1)
+            for c in range(3):
+                col = 3 * part + c
+                nc.tensor.transpose(bank[:, c * P : (c + 1) * P], g_words[:, col : col + 1].to_broadcast([P, P]), ident[:])
+            done.add(("g", part))
+            return True
+
+        def g_out(eng, part):
+            if ("g", part) not in done:
+                return False
+            words = g_all[:].bitcast(F32).rearrange("p (a n c) -> p a n c", a=2, c=3)
+            copy(eng, words[:, part], have["g", part][:, : 3 * P].rearrange("p (c n) -> p n c", c=3))
+            used(("g", part))
+            filled("gall", 1, 2)
+            return True
+
+        def gain(eng, h, q, t):
+            if ("in", "d", h, q) not in done or "gall" not in done or not free["gd"]:
+                return False
+            tile = take("gd", ("gd", h, q, t), 1)
+            builder = nc.vector if eng == "V" else nc.gpsimd
+            builder.tensor_tensor(out=tile[:], in0=have["in", "d", h, q][:, blk(t)], in1=g_all[:, blk(q)], op=MULT)
+            used(("in", "d", h, q))
+            done.add(("gd", h, q, t))
+            return True
+
+        def evac(eng, h, q, t):
+            if ("du", h, q, t) not in done or ("gd", h, q, t) not in done:
+                return False
+            dst = obtain("dp", ("in", "dp", h, q), 2 + W)
+            if dst is None:
+                return False
+            nc.vector.tensor_tensor(
+                out=dst[:, blk(t)].rearrange("p (u m e) -> p u m e", u=2, e=2),
+                in0=have["du", h, q, t][:].rearrange("p (m u e) -> p u m e", u=2, e=2),
+                in1=have["gd", h, q, t][:].rearrange("p (m u e) -> p u m e", u=2, e=2),
+                op=MULT,
+            )
+            used(("du", h, q, t))
+            used(("gd", h, q, t))
+            filled(("part", t // 2, "dp", h, q), 1, 2)
+            filled(("in", "dp", h, q), 1, 4)
+            return True
+
+        def out(eng, kind, i, j):
+            if (kind, i, j) not in done:
+                return False
+            res = take("res", "res", 1)
+            bank = have[kind, i, j]
+            if kind == "dm":
+                copy(eng, res[:].rearrange("p (m u e) -> p m u e", u=2, e=2), bank[:].rearrange("p (u m e) -> p m u e", u=2, e=2))
+                nc.sync.dma_start(out=out_1[j * P : (j + 1) * P, blk(i)], in_=res[:])
+            else:
+                copy(eng, res[:], bank[:])
+                nc.sync.dma_start(out=rows4(out_0[blk(i), :])[:, j, :], in_=res[:])
+            used((kind, i, j))
+            used("res")
+            return True
+
+        V, S, T, G = [], [], [], []
+        def turns(key):
+            return [(turn, key, 0), (turn, key, 1)]
+
+        def pairs2(key):
+            return [(pairs, key, 0), (pairs, key, 1)]
+
+        def tile4(h, q, t):
+            return [(du, h, q, t, k) for k in range(4)]
+
+        def wv(key, lo=0, hi=W):
+            return [(weave, key, lo, hi)] if lo < hi else []
+
+        def qq(key):
+            return [(quant, key)]
+
+        def wdp(h, q):
+            return ("w", "dp", h, q)
+
+        units = [(h, q) for q in range(3) for h in range(2)]
+
+        def ge(n):
+            steps = [(evac,) + units[n // 4] + (n % 4,)]
+            if n + 2 < 24:
+                steps.append((gain,) + units[(n + 2) // 4] + ((n + 2) % 4,))
+            return steps
+
+        def tl(n):
+            return tile4(*units[n // 4], n % 4)
+
+        HV = 320
+        for k in range(4):
+            V += wv(("z", 0, k), 0, HV)
+            S += wv(("z", 0, k), HV, W) + pairs2(("ds", 0, k))
+            if k > 0:
+                V += qq(("ds", 0, k - 1))
+            V += qq(("z", 0, k))
+            T += turns(("ds", 0, k))
+            if k == 1:
+                T += [(spread, 0), (spread, 1)]
+                S += [(g_out, 0), (g_out, 1)]
+            if k > 0:
+                T += [(du, 0, 0, k - 1, kk) for kk in range(k)] + [(du, 0, 0, t, k) for t in range(k)]
+        Z1 = 64
+        def dxs(h, ts=range(4)):
+            return [(dx, h, t, q) for t in ts for q in range(3)]
+
+        def dms(q, cs=range(4)):
+            return [(dm, q, c, h) for c in cs for h in range(2)]
+
+        V += wv(("z", 1, 0), 0, Z1) + qq(("ds", 0, 3)) + [(gain, 0, 0, 0), (gain, 0, 0, 1)] + ge(0) + qq(("z", 1, 0)) + ge(1)
+        V += qq(("ds", 1, 0)) + ge(2) + qq(("ds", 1, 1)) + wv(("z", 1, 1), 0, Z1) + ge(3) + ge(4) + qq(("z", 1, 1)) + qq(("ds", 1, 2))
+        V += ge(5) + qq(("ds", 1, 3)) + wv(("z", 1, 2), 0, Z1) + wv(("z", 1, 3), 0, Z1) + ge(6) + qq(("z", 1, 2)) + ge(7) + qq(("z", 1, 3))
+        S += wv(("z", 1, 0), Z1, W) + pairs2(("ds", 1, 0)) + pairs2(("ds", 1, 1)) + wv(("z", 1, 1), Z1, W) + pairs2(("ds", 1, 2))
+        S += pairs2(("ds", 1, 3)) + wv(("z", 1, 2), Z1, W) + wv(("z", 1, 3), Z1, W) + pairs2(("dp", 0, 0))
+        T += turns(("ds", 1, 0)) + tl(3) + turns(("ds", 1, 1)) + tl(4) + turns(("ds", 1, 2)) + turns(("ds", 1, 3)) + tl(5) + tl(6)
+        T += turns(("dp", 0, 0)) + tl(7) + [(du, 0, 1, t, k) for k in range(4) for t in range(2)]
+        S += wv(("z", 2, 0)) + pairs2(("dp", 1, 0)) + wv(("z", 2, 1)) + wv(("z", 2, 2)) + wv(("z", 2, 3)) + pairs2(("dp", 0, 1))
+        S += pairs2(("m", 0)) + pairs2(("m", 1)) + wv(wdp(0, 0)) + pairs2(("dp", 1, 1)) + pairs2(("m", 2)) + wv(("x", 0)) + pairs2(("dp", 0, 2)) + wv(("x", 1))
+        V += ge(8) + qq(("dp", 0, 0)) + ge(9) + qq(("z", 2, 0)) + ge(10) + ge(11) + qq(("z", 2, 1)) + ge(12) + qq(("dp", 1, 0)) + ge(13) + qq(("z", 2, 2))
+        V += ge(14) + qq(("z", 2, 3)) + ge(15) + qq(("dp", 0, 1)) + ge(16) + qq(("m", 0)) + ge(17) + qq(("m", 1)) + ge(18) + ge(19) + qq(("dp", 1, 1)) + ge(20) + qq(("m", 2)) + ge(21) + qq(("dp", 0, 2)) + ge(22) + ge(23)
+        T += tl(10) + turns(("dp", 1, 0)) + tl(11) + tl(12) + tl(13) + turns(("dp", 0, 1)) + tl(14) + tl(15)
+        T += turns(("m", 0)) + tl(16) + turns(("m", 1)) + tl(17) + tl(18) + turns(("dp", 1, 1)) + tl(19) + turns(("m", 2)) + tl(20) + tl(21) + turns(("dp", 0, 2)) + tl(22) + tl(23)
+        T += dxs(0, range(2)) + turns(("dp", 1, 2)) + dxs(0, range(2, 4)) + dms(0, range(2)) + dxs(1, range(2)) + dms(0, range(2, 4)) + dxs(1, range(2, 4)) + dms(1) + dms(2)
+        V += wv(wdp(1, 0)) + qq(wdp(0, 0)) + qq(("x", 0)) + qq(wdp(1, 0)) + qq(("x", 1)) + wv(wdp(0, 1)) + qq(("dp", 1, 2))
+        V += wv(wdp(1, 1)) + qq(wdp(0, 1)) + wv(wdp(0, 2)) + qq(wdp(1, 1)) + wv(wdp(1, 2)) + qq(wdp(0, 2)) + qq(wdp(1, 2))
+        S += [(out, "dx", 0, t) for t in range(2)] + pairs2(("dp", 1, 2)) + [(out, "dx", 0, t) for t in range(2, 4)]
+        S += [(out, "dm", 0, 0), (out, "dm", 0, 1), (out, "dx", 1, 0), (out, "dx", 1, 1), (out, "dm", 0, 2), (out, "dm", 0, 3), (out, "dx", 1, 2), (out, "dx", 1, 3)]
+        S += [(out, "dm", 1, c) for c in range(4)]
+        for t in range(4):
+            (S if t % 2 else V).append((out, "dm", 2, t))
+
+        load_more()
+        queues = {"V": V, "S": S, "T": T, "G": G}
+        while any(queues.values()):
+            moved = False
+            for eng, steps in queues.items():
+                if steps and steps[0][0](eng, *steps[0][1:]):
+                    steps.pop(0)
+                    moved = True
+            assert moved, str([s[0][1:] for s in queues.values() if s])

@@ -44,6 +44,10 @@ def tile_pair_score_metric_backward_s6_kernel(tc, ds, z, d, g, metric, x, out_0,
         ident = tiles("ident", 1, P, F32)[0]
         g_words = tiles("gw", 1, 6, F32)[0]
         g_all = tiles("gall", 1, F, BF16)[0]
+        nc.scalar.dma_start(
+            out=g_words[:].rearrange("p (a c) -> p a c", a=2),
+            in_=g.bitcast(F32).rearrange("(a p c) -> p a c", a=2, c=3),
+        )
         make_identity(nc, ident[:])
 
         have = {}
@@ -80,7 +84,7 @@ def tile_pair_score_metric_backward_s6_kernel(tc, ds, z, d, g, metric, x, out_0,
                 return metric[:, blk(key[1])].rearrange("(j p) w -> p j w", j=4), 2
             return rows4(z[blk(key[2]), blk(key[1])]), W
 
-        order = [key for k in range(4) for key in (("z", 0, k), ("ds", 0, k))] + [("z", 1, 0), ("d", 0, 0), ("ds", 1, 0), ("ds", 1, 1), ("z", 1, 1), ("d", 1, 0), ("ds", 1, 2), ("ds", 1, 3), ("z", 1, 2), ("z", 1, 3), ("d", 0, 1), ("z", 2, 0), ("d", 1, 1)] + [("z", 2, k) for k in range(1, 4)] + [("d", 0, 2)] + [("m", q) for q in range(3)] + [("d", 1, 2), ("x", 0), ("x", 1)]
+        order = [("ds", 0, 0), ("ds", 0, 1), ("z", 0, 0), ("z", 0, 1), ("ds", 0, 2), ("ds", 0, 3), ("z", 0, 2), ("ds", 1, 0), ("z", 0, 3), ("d", 0, 0), ("ds", 1, 1), ("z", 1, 0), ("ds", 1, 2), ("d", 1, 0), ("z", 1, 1), ("ds", 1, 3), ("z", 1, 2), ("z", 1, 3), ("d", 0, 1), ("z", 2, 0), ("d", 1, 1)] + [("z", 2, k) for k in range(1, 4)] + [("d", 0, 2)] + [("m", q) for q in range(3)] + [("d", 1, 2), ("x", 0), ("x", 1)]
 
         def load_more():
             while order and free["raw"]:
@@ -89,11 +93,6 @@ def tile_pair_score_metric_backward_s6_kernel(tc, ds, z, d, g, metric, x, out_0,
                 tile = take("raw", ("in",) + key, uses)
                 nc.sync.dma_start(out=tile[:].rearrange("p (j w) -> p j w", j=4), in_=src)
                 done.add(("in",) + key)
-                if key == ("ds", 0, 0):
-                    nc.sync.dma_start(
-                        out=g_words[:].rearrange("p (a c) -> p a c", a=2),
-                        in_=g.bitcast(F32).rearrange("(a p c) -> p a c", a=2, c=3),
-                    )
 
         def copy(eng, out, in_):
             if eng == "V":
@@ -254,18 +253,56 @@ def tile_pair_score_metric_backward_s6_kernel(tc, ds, z, d, g, metric, x, out_0,
             return True
 
         def out(eng, kind, i, j):
-            if (kind, i, j) not in done:
+            if (kind, i, j) not in done or not free["res"]:
                 return False
-            res = take("res", "res", 1)
+            res = take("res", ("res", kind, i, j), 1)
             bank = have[kind, i, j]
             if kind == "dm":
                 copy(eng, res[:].rearrange("p (m u e) -> p m u e", u=2, e=2), bank[:].rearrange("p (u m e) -> p m u e", u=2, e=2))
-                nc.sync.dma_start(out=out_1[j * P : (j + 1) * P, blk(i)], in_=res[:])
             else:
                 copy(eng, res[:], bank[:])
-                nc.sync.dma_start(out=rows4(out_0[blk(i), :])[:, j, :], in_=res[:])
             used((kind, i, j))
-            used("res")
+            done.add(("res", kind, i, j))
+            return True
+
+        def store(eng, kind, i, j):
+            if ("res", kind, i, j) not in done:
+                return False
+            dst = out_1[j * P : (j + 1) * P, blk(i)] if kind == "dm" else rows4(out_0[blk(i), :])[:, j, :]
+            nc.sync.dma_start(out=dst, in_=have["res", kind, i, j][:])
+            used(("res", kind, i, j))
+            return True
+
+        def warm_prep(eng):
+            zeros = take("grp", "zeros", 1)
+            nc.vector.memset(zeros[:].bitcast(U32), 0)
+            a = take("e5", "warm5", 1)
+            b = take("e4", "warm4", 1)
+            take("bank", "warm", 1)
+            nc.vector.quantize_mx(out=a[0][:, :P].bitcast(E5M2), scales=a[1][:, :P], in_=zeros[:, :W])
+            nc.vector.quantize_mx(out=b[0][:].bitcast(E4M3), scales=b[1][:], in_=zeros[:])
+            used("zeros")
+            done.add("warm")
+            return True
+
+        def warm(eng, count, last):
+            if "warm" not in done:
+                return False
+            a, b = have["warm5"], have["warm4"]
+            for i in range(count):
+                nc.tensor.matmul_mx(
+                    out=have["warm"][:],
+                    lhsT=a[0][:, :P].bitcast(E5M2),
+                    lhsT_scale=a[1][:, :P],
+                    rhs=b[0][:].bitcast(E4M3),
+                    rhs_scale=b[1][:],
+                    start=True,
+                    stop=True,
+                )
+            if last:
+                used("warm5")
+                used("warm4")
+                used("warm")
             return True
 
         V, S, T, G = [], [], [], []
@@ -298,50 +335,41 @@ def tile_pair_score_metric_backward_s6_kernel(tc, ds, z, d, g, metric, x, out_0,
         def tl(n):
             return tile4(*units[n // 4], n % 4)
 
-        HV = 320
-        for k in range(4):
-            V += wv(("z", 0, k), 0, HV)
-            S += wv(("z", 0, k), HV, W) + pairs2(("ds", 0, k))
-            if k > 0:
-                V += qq(("ds", 0, k - 1))
-            V += qq(("z", 0, k))
-            T += turns(("ds", 0, k))
-            if k == 1:
-                T += [(spread, 0), (spread, 1)]
-                S += [(g_out, 0), (g_out, 1)]
-            if k > 0:
-                T += [(du, 0, 0, k - 1, kk) for kk in range(k)] + [(du, 0, 0, t, k) for t in range(k)]
-        Z1 = 64
         def dxs(h, ts=range(4)):
             return [(dx, h, t, q) for t in ts for q in range(3)]
 
         def dms(q, cs=range(4)):
             return [(dm, q, c, h) for c in cs for h in range(2)]
 
-        V += wv(("z", 1, 0), 0, Z1) + qq(("ds", 0, 3)) + [(gain, 0, 0, 0), (gain, 0, 0, 1)] + ge(0) + qq(("z", 1, 0)) + ge(1)
-        V += qq(("ds", 1, 0)) + ge(2) + qq(("ds", 1, 1)) + wv(("z", 1, 1), 0, Z1) + ge(3) + ge(4) + qq(("z", 1, 1)) + qq(("ds", 1, 2))
-        V += ge(5) + qq(("ds", 1, 3)) + wv(("z", 1, 2), 0, Z1) + wv(("z", 1, 3), 0, Z1) + ge(6) + qq(("z", 1, 2)) + ge(7) + qq(("z", 1, 3))
-        S += wv(("z", 1, 0), Z1, W) + pairs2(("ds", 1, 0)) + pairs2(("ds", 1, 1)) + wv(("z", 1, 1), Z1, W) + pairs2(("ds", 1, 2))
-        S += pairs2(("ds", 1, 3)) + wv(("z", 1, 2), Z1, W) + wv(("z", 1, 3), Z1, W) + pairs2(("dp", 0, 0))
-        T += turns(("ds", 1, 0)) + tl(3) + turns(("ds", 1, 1)) + tl(4) + turns(("ds", 1, 2)) + turns(("ds", 1, 3)) + tl(5) + tl(6)
-        T += turns(("dp", 0, 0)) + tl(7) + [(du, 0, 1, t, k) for k in range(4) for t in range(2)]
-        S += wv(("z", 2, 0)) + pairs2(("dp", 1, 0)) + wv(("z", 2, 1)) + wv(("z", 2, 2)) + wv(("z", 2, 3)) + pairs2(("dp", 0, 1))
-        S += pairs2(("m", 0)) + pairs2(("m", 1)) + wv(wdp(0, 0)) + pairs2(("dp", 1, 1)) + pairs2(("m", 2)) + wv(("x", 0)) + pairs2(("dp", 0, 2)) + wv(("x", 1))
-        V += ge(8) + qq(("dp", 0, 0)) + ge(9) + qq(("z", 2, 0)) + ge(10) + ge(11) + qq(("z", 2, 1)) + ge(12) + qq(("dp", 1, 0)) + ge(13) + qq(("z", 2, 2))
-        V += ge(14) + qq(("z", 2, 3)) + ge(15) + qq(("dp", 0, 1)) + ge(16) + qq(("m", 0)) + ge(17) + qq(("m", 1)) + ge(18) + ge(19) + qq(("dp", 1, 1)) + ge(20) + qq(("m", 2)) + ge(21) + qq(("dp", 0, 2)) + ge(22) + ge(23)
-        T += tl(10) + turns(("dp", 1, 0)) + tl(11) + tl(12) + tl(13) + turns(("dp", 0, 1)) + tl(14) + tl(15)
-        T += turns(("m", 0)) + tl(16) + turns(("m", 1)) + tl(17) + tl(18) + turns(("dp", 1, 1)) + tl(19) + turns(("m", 2)) + tl(20) + tl(21) + turns(("dp", 0, 2)) + tl(22) + tl(23)
-        T += dxs(0, range(2)) + turns(("dp", 1, 2)) + dxs(0, range(2, 4)) + dms(0, range(2)) + dxs(1, range(2)) + dms(0, range(2, 4)) + dxs(1, range(2, 4)) + dms(1) + dms(2)
-        V += wv(wdp(1, 0)) + qq(wdp(0, 0)) + qq(("x", 0)) + qq(wdp(1, 0)) + qq(("x", 1)) + wv(wdp(0, 1)) + qq(("dp", 1, 2))
-        V += wv(wdp(1, 1)) + qq(wdp(0, 1)) + wv(wdp(0, 2)) + qq(wdp(1, 1)) + wv(wdp(1, 2)) + qq(wdp(0, 2)) + qq(wdp(1, 2))
-        S += [(out, "dx", 0, t) for t in range(2)] + pairs2(("dp", 1, 2)) + [(out, "dx", 0, t) for t in range(2, 4)]
-        S += [(out, "dm", 0, 0), (out, "dm", 0, 1), (out, "dx", 1, 0), (out, "dx", 1, 1), (out, "dm", 0, 2), (out, "dm", 0, 3), (out, "dx", 1, 2), (out, "dx", 1, 3)]
-        S += [(out, "dm", 1, c) for c in range(4)]
+
+        WARM = [2, 2, 2, 0]
+        T += [(spread, 0), (spread, 1)] + turns(("ds", 0, 0)) + turns(("ds", 0, 1))
+        T += turns(("ds", 0, 2)) + [(du, 0, 0, t, 0) for t in range(2)] + turns(("ds", 0, 3)) + [(du, 0, 0, t, 1) for t in range(2)] + [(du, 0, 0, 2, k) for k in range(2)]
+        T += turns(("ds", 1, 0)) + [(du, 0, 0, 3, k) for k in range(2)] + [(du, 0, 0, t, 2) for t in range(4)] + turns(("ds", 1, 1)) + [(du, 0, 0, t, 3) for t in range(4)]
+        S += [(g_out, 0), (g_out, 1)] + pairs2(("ds", 0, 0)) + pairs2(("ds", 0, 1)) + wv(("z", 0, 1), 256) + pairs2(("ds", 0, 2)) + pairs2(("ds", 0, 3)) + pairs2(("ds", 1, 0)) + wv(("z", 0, 3), 512)
+        V += qq(("ds", 0, 0)) + wv(("z", 0, 0)) + qq(("ds", 0, 1)) + qq(("z", 0, 0)) + wv(("z", 0, 1), 0, 256) + qq(("z", 0, 1)) + qq(("ds", 0, 2)) + wv(("z", 0, 2)) + qq(("ds", 0, 3)) + qq(("z", 0, 2))
+        V += wv(("z", 0, 3), 0, 512) + qq(("ds", 1, 0)) + qq(("z", 0, 3)) + [(gain, 0, 0, t) for t in range(2)]
+
+        S += pairs2(("ds", 1, 1)) + wv(("z", 1, 0)) + pairs2(("ds", 1, 2)) + wv(("z", 1, 1)) + pairs2(("ds", 1, 3)) + wv(("z", 1, 2)) + wv(("z", 1, 3), 256) + pairs2(("dp", 0, 0))
+        V += ge(0) + qq(("ds", 1, 1)) + ge(1) + ge(2) + qq(("z", 1, 0)) + ge(3) + qq(("ds", 1, 2)) + ge(4) + qq(("z", 1, 1)) + ge(5) + qq(("ds", 1, 3)) + ge(6) + wv(("z", 1, 3), 0, 256) + qq(("z", 1, 2)) + ge(7) + qq(("z", 1, 3))
+        T += tl(4) + turns(("ds", 1, 2)) + tl(5) + turns(("ds", 1, 3)) + tl(6) + [(du, 0, 1, t, k) for k in range(2) for t in range(2)] + tl(7) + turns(("dp", 0, 0))
+        T += [(du, 0, 1, t, 2) for t in range(2)] + [(du, 0, 1, 2, k) for k in range(3)] + [(du, 0, 1, t, 3) for t in range(3)] + tl(11)
+        S += wv(("z", 2, 0)) + wv(("z", 2, 1)) + pairs2(("dp", 1, 0)) + wv(("z", 2, 2)) + wv(("z", 2, 3)) + pairs2(("dp", 0, 1)) + pairs2(("m", 0))
+        V += ge(8) + qq(("dp", 0, 0)) + ge(9) + qq(("z", 2, 0)) + ge(10) + qq(("z", 2, 1)) + ge(11) + ge(12) + qq(("z", 2, 2)) + ge(13) + qq(("dp", 1, 0)) + ge(14) + qq(("z", 2, 3)) + ge(15)
+        T += tl(12) + turns(("dp", 1, 0)) + tl(13) + tl(14) + turns(("dp", 0, 1)) + tl(15) + [(du, 0, 2, t, k) for k in range(2) for t in range(2)] + turns(("m", 0)) + [(du, 0, 2, t, 2) for t in range(2)] + turns(("m", 1))
+        T += [(du, 0, 2, t, 3) for t in range(2)] + tl(18) + turns(("dp", 1, 1)) + tl(19) + turns(("m", 2)) + tl(20) + tl(21) + turns(("dp", 0, 2)) + tl(22) + tl(23)
+        S += pairs2(("m", 1)) + wv(wdp(0, 0)) + pairs2(("dp", 1, 1)) + pairs2(("m", 2)) + wv(("x", 0)) + pairs2(("dp", 0, 2)) + wv(("x", 1))
+        V += qq(("dp", 0, 1)) + ge(16) + qq(("m", 0)) + ge(17) + qq(("m", 1)) + ge(18) + ge(19) + qq(("dp", 1, 1)) + ge(20) + qq(("m", 2)) + ge(21) + qq(wdp(0, 0)) + ge(22) + qq(("dp", 0, 2)) + ge(23)
+        T += dxs(0, range(2)) + turns(("dp", 1, 2)) + dxs(0, range(2, 4)) + dms(0) + dxs(1) + dms(1) + dms(2)
+        V += wv(wdp(1, 0)) + qq(("x", 0)) + qq(wdp(1, 0)) + qq(("x", 1)) + qq(("dp", 1, 2)) + wv(wdp(0, 1)) + wv(wdp(1, 1)) + qq(wdp(0, 1)) + qq(wdp(1, 1))
+        V += wv(wdp(0, 2)) + wv(wdp(1, 2)) + qq(wdp(0, 2)) + qq(wdp(1, 2))
+        S += pairs2(("dp", 1, 2)) + [(out, "dx", 0, t) for t in range(4)] + [(out, "dm", 0, t) for t in range(4)] + [(out, "dx", 1, t) for t in range(4)] + [(out, "dm", 1, t) for t in range(4)]
         for t in range(4):
             (S if t % 2 else V).append((out, "dm", 2, t))
 
         load_more()
-        queues = {"V": V, "S": S, "T": T, "G": G}
+        Y = [(store, "dm") + s[1:3] if s[0] is dm else (store, "dx") + s[1:3] for s in T if (s[0] is dm and s[3] == 1) or (s[0] is dx and s[3] == 2)]
+        queues = {"V": V, "S": S, "T": T, "G": G, "Y": Y}
         while any(queues.values()):
             moved = False
             for eng, steps in queues.items():

@@ -29,17 +29,17 @@ def tile_pair_score_metric_backward_s6_kernel(tc, ds, z, d, g, metric, x, out_0,
             return [sb.tile([P, width], dtype, name="%s%d" % (name, i), align_bytes=64) for i in range(count)]
 
         def operands(name, count):
-            return list(zip(tiles(name + "c", count, W, U32), tiles(name + "s", count, W, U8)))
+            return list(zip(tiles(name + "c", count, 2 * W, U32), tiles(name + "s", count, 2 * W, U8)))
 
         free = {
             "bank": [ps.tile([P, W], F32, name="bank%d" % i) for i in range(8)],
             "raw": tiles("raw", 16, 4 * W, BF16),
-            "grp": tiles("grp", 7, 4 * W, BF16),
-            "gd": tiles("gd", 4, W, F32),
+            "grp": tiles("grp", 5, 8 * W, BF16),
+            "gd": tiles("gd", 2, 4 * W, F32),
             "dp": tiles("dp", 6, 4 * W, BF16),
             "res": tiles("res", 8, W, F32),
-            "e4": operands("e4", 13),
-            "e5": operands("e5", 18),
+            "e4": operands("e4", 5),
+            "e5": operands("e5", 8),
         }
         ident = tiles("ident", 1, P, F32)[0]
         g_words = tiles("gw", 1, 6, F32)[0]
@@ -84,7 +84,7 @@ def tile_pair_score_metric_backward_s6_kernel(tc, ds, z, d, g, metric, x, out_0,
                 return metric[:, blk(key[1])].rearrange("(j p) w -> p j w", j=4), 2
             return rows4(z[blk(key[2]), blk(key[1])]), W
 
-        order = [("ds", 0, 0), ("ds", 0, 1), ("z", 0, 0), ("z", 0, 1), ("ds", 0, 2), ("ds", 0, 3), ("z", 0, 2), ("ds", 1, 0), ("z", 0, 3), ("d", 0, 0), ("ds", 1, 1), ("z", 1, 0), ("ds", 1, 2), ("d", 1, 0), ("z", 1, 1), ("ds", 1, 3), ("z", 1, 2), ("z", 1, 3), ("d", 0, 1), ("z", 2, 0), ("d", 1, 1)] + [("z", 2, k) for k in range(1, 4)] + [("d", 0, 2)] + [("m", q) for q in range(3)] + [("d", 1, 2), ("x", 0), ("x", 1)]
+        order = [key for k in range(4) for key in (("z", 0, k), ("ds", 0, k))] + [("z", 1, 0), ("d", 0, 0), ("ds", 1, 0), ("ds", 1, 1), ("z", 1, 1), ("ds", 1, 2), ("d", 1, 0), ("ds", 1, 3), ("z", 1, 2), ("z", 1, 3), ("d", 0, 1), ("z", 2, 0), ("d", 1, 1)] + [("z", 2, k) for k in range(1, 4)] + [("d", 0, 2), ("m", 0), ("m", 1), ("d", 1, 2), ("m", 2), ("x", 0), ("x", 1)]
 
         def load_more():
             while order and free["raw"]:
@@ -112,15 +112,27 @@ def tile_pair_score_metric_backward_s6_kernel(tc, ds, z, d, g, metric, x, out_0,
             if left["fill", key] == total:
                 done.add(key)
 
+        def pair_of(key):
+            if key[0] in ("dp", "w"):
+                return key[:-2] + key[-1:], key[-2], 2
+            if key == ("m", 2):
+                return ("m", 1), 0, 1
+            return key[:-1] + (key[-1] // 2,), key[-1] % 2, 2
+
+        def staging(key):
+            pair, side, count = pair_of(key)
+            tile = obtain("grp", ("stage",) + pair, count)
+            return None if tile is None else tile[:, side * 4 * W : (side + 1) * 4 * W]
+
         def weave(eng, key, lo, hi):
             src = ("in",) + key[1:] if key[0] == "w" else ("in",) + key
             if src not in done:
                 return False
-            dst = obtain("grp", ("grp",) + key, 1)
+            dst = staging(key)
             if dst is None:
                 return False
             rows = have[src][:].rearrange("p (t c i) -> p c t i", t=4, i=4)
-            side = dst[:].rearrange("p (c i t) -> p c t i", t=4, i=4)
+            side = dst.rearrange("p (c i t) -> p c t i", t=4, i=4)
             copy(eng, side[:, lo // 4 : hi // 4], rows[:, lo // 4 : hi // 4])
             used(src, hi - lo)
             filled(("grp",) + key, hi - lo, W)
@@ -128,16 +140,23 @@ def tile_pair_score_metric_backward_s6_kernel(tc, ds, z, d, g, metric, x, out_0,
 
         uses_of = {"z": 8, "ds": 12, "m": 8, "x": 12, "dp": 4, "w": 4}
 
-        def quant(eng, key):
-            kind = "e4" if key[0] in ("z", "m", "x") else "e5"
-            if ("grp",) + key not in done or not free[kind]:
+        def quant(eng, *keys):
+            kind = "e4" if keys[0][0] in ("z", "m", "x") else "e5"
+            if any(("grp",) + key not in done for key in keys):
                 return False
-            operand = take(kind, ("q",) + key, uses_of[key[0]])
+            pair, side, count = pair_of(keys[0])
+            operand = obtain(kind, ("q",) + pair, count * uses_of[pair[0]])
+            if operand is None:
+                return False
+            cols = slice(side * W, (side + len(keys)) * W)
             nc.vector.quantize_mx(
-                out=operand[0][:].bitcast(E4M3 if kind == "e4" else E5M2), scales=operand[1][:], in_=have[("grp",) + key][:]
+                out=operand[0][:, cols].bitcast(E4M3 if kind == "e4" else E5M2),
+                scales=operand[1][:, cols],
+                in_=have[("stage",) + pair][:, side * 4 * W : (side + len(keys)) * 4 * W],
             )
-            used(("grp",) + key)
-            done.add(("q",) + key)
+            used(("stage",) + pair, len(keys))
+            for key in keys:
+                done.add(("q",) + key)
             return True
 
         def turn(eng, key, half):
@@ -162,12 +181,12 @@ def tile_pair_score_metric_backward_s6_kernel(tc, ds, z, d, g, metric, x, out_0,
         def pairs(eng, key, half):
             if ("t", half) + key not in done:
                 return False
-            dst = obtain("grp", ("grp",) + key, 1)
+            dst = staging(key)
             if dst is None:
                 return False
             copy(
                 eng,
-                dst[:].bitcast(F32)[:, blk(half)].rearrange("p (j r u) -> p j r u", j=2, u=2),
+                dst.bitcast(F32)[:, blk(half)].rearrange("p (j r u) -> p j r u", j=2, u=2),
                 have[("t", half) + key][:].rearrange("p (j u r) -> p j r u", j=2, u=2),
             )
             used(("t", half) + key)
@@ -180,19 +199,20 @@ def tile_pair_score_metric_backward_s6_kernel(tc, ds, z, d, g, metric, x, out_0,
             bank = obtain("bank", acc, 1)
             if bank is None:
                 return False
-            cols = slice(col * P, (col + 1) * P)
-            a, b = have[("q",) + still], have[("q",) + moving]
+            (pa, sa), (pb, sm) = pair_of(still)[:2], pair_of(moving)[:2]
+            cols = slice(sa * W + col * P, sa * W + (col + 1) * P)
+            a, b = have[("q",) + pa], have[("q",) + pb]
             nc.tensor.matmul_mx(
                 out=bank[:],
                 lhsT=a[0][:, cols].bitcast(E4M3 if still[0] == "x" else E5M2),
                 lhsT_scale=a[1][:, cols],
-                rhs=b[0][:].bitcast(E5M2 if still[0] == "x" else E4M3),
-                rhs_scale=b[1][:],
+                rhs=b[0][:, blk(sm)].bitcast(E5M2 if still[0] == "x" else E4M3),
+                rhs_scale=b[1][:, blk(sm)],
                 start=step == 0,
                 stop=step == steps - 1,
             )
-            used(("q",) + still)
-            used(("q",) + moving)
+            used(("q",) + pa)
+            used(("q",) + pb)
             filled(acc, 1, steps)
             return True
 
@@ -224,14 +244,21 @@ def tile_pair_score_metric_backward_s6_kernel(tc, ds, z, d, g, metric, x, out_0,
             filled("gall", 1, 2)
             return True
 
-        def gain(eng, h, q, t):
-            if ("in", "d", h, q) not in done or "gall" not in done or not free["gd"]:
+        def gain(eng, h, q, t0, t1):
+            if ("in", "d", h, q) not in done or "gall" not in done:
                 return False
-            tile = take("gd", ("gd", h, q, t), 1)
-            builder = nc.vector if eng == "V" else nc.gpsimd
-            builder.tensor_tensor(out=tile[:], in0=have["in", "d", h, q][:, blk(t)], in1=g_all[:, blk(q)], op=MULT)
-            used(("in", "d", h, q))
-            done.add(("gd", h, q, t))
+            tile = obtain("gd", ("gd", h, q), 4)
+            if tile is None:
+                return False
+            nc.vector.tensor_tensor(
+                out=tile[:].rearrange("p (t f) -> p t f", t=4)[:, t0:t1],
+                in0=have["in", "d", h, q][:].rearrange("p (t f) -> p t f", t=4)[:, t0:t1],
+                in1=g_all[:, blk(q)].unsqueeze(1).to_broadcast([P, t1 - t0, W]),
+                op=MULT,
+            )
+            used(("in", "d", h, q), t1 - t0)
+            for t in range(t0, t1):
+                done.add(("gd", h, q, t))
             return True
 
         def evac(eng, h, q, t):
@@ -243,11 +270,11 @@ def tile_pair_score_metric_backward_s6_kernel(tc, ds, z, d, g, metric, x, out_0,
             nc.vector.tensor_tensor(
                 out=dst[:, blk(t)].rearrange("p (u m e) -> p u m e", u=2, e=2),
                 in0=have["du", h, q, t][:].rearrange("p (m u e) -> p u m e", u=2, e=2),
-                in1=have["gd", h, q, t][:].rearrange("p (m u e) -> p u m e", u=2, e=2),
+                in1=have["gd", h, q][:, blk(t)].rearrange("p (m u e) -> p u m e", u=2, e=2),
                 op=MULT,
             )
             used(("du", h, q, t))
-            used(("gd", h, q, t))
+            used(("gd", h, q))
             filled(("part", t // 2, "dp", h, q), 1, 2)
             filled(("in", "dp", h, q), 1, 4)
             return True
@@ -275,12 +302,12 @@ def tile_pair_score_metric_backward_s6_kernel(tc, ds, z, d, g, metric, x, out_0,
 
         def warm_prep(eng):
             zeros = take("grp", "zeros", 1)
-            nc.vector.memset(zeros[:].bitcast(U32), 0)
+            nc.vector.memset(zeros[:, : 4 * W].bitcast(U32), 0)
             a = take("e5", "warm5", 1)
             b = take("e4", "warm4", 1)
             take("bank", "warm", 1)
             nc.vector.quantize_mx(out=a[0][:, :P].bitcast(E5M2), scales=a[1][:, :P], in_=zeros[:, :W])
-            nc.vector.quantize_mx(out=b[0][:].bitcast(E4M3), scales=b[1][:], in_=zeros[:])
+            nc.vector.quantize_mx(out=b[0][:, :W].bitcast(E4M3), scales=b[1][:, :W], in_=zeros[:, : 4 * W])
             used("zeros")
             done.add("warm")
             return True
@@ -294,8 +321,8 @@ def tile_pair_score_metric_backward_s6_kernel(tc, ds, z, d, g, metric, x, out_0,
                     out=have["warm"][:],
                     lhsT=a[0][:, :P].bitcast(E5M2),
                     lhsT_scale=a[1][:, :P],
-                    rhs=b[0][:].bitcast(E4M3),
-                    rhs_scale=b[1][:],
+                    rhs=b[0][:, :W].bitcast(E4M3),
+                    rhs_scale=b[1][:, :W],
                     start=True,
                     stop=True,
                 )
@@ -318,19 +345,19 @@ def tile_pair_score_metric_backward_s6_kernel(tc, ds, z, d, g, metric, x, out_0,
         def wv(key, lo=0, hi=W):
             return [(weave, key, lo, hi)] if lo < hi else []
 
-        def qq(key):
-            return [(quant, key)]
+        def qq(*keys):
+            return [(quant,) + keys]
 
         def wdp(h, q):
             return ("w", "dp", h, q)
 
         units = [(h, q) for q in range(3) for h in range(2)]
 
-        def ge(n):
-            steps = [(evac,) + units[n // 4] + (n % 4,)]
-            if n + 2 < 24:
-                steps.append((gain,) + units[(n + 2) // 4] + ((n + 2) % 4,))
-            return steps
+        def ev(*ns):
+            return [(evac,) + units[n // 4] + (n % 4,) for n in ns]
+
+        def gn(u, t0=0, t1=4):
+            return [(gain,) + units[u] + (t0, t1)]
 
         def tl(n):
             return tile4(*units[n // 4], n % 4)
@@ -341,29 +368,38 @@ def tile_pair_score_metric_backward_s6_kernel(tc, ds, z, d, g, metric, x, out_0,
         def dms(q, cs=range(4)):
             return [(dm, q, c, h) for c in cs for h in range(2)]
 
+        def Z(q, k):
+            return ("z", q, k)
 
-        WARM = [2, 2, 2, 0]
-        T += [(spread, 0), (spread, 1)] + turns(("ds", 0, 0)) + turns(("ds", 0, 1))
-        T += turns(("ds", 0, 2)) + [(du, 0, 0, t, 0) for t in range(2)] + turns(("ds", 0, 3)) + [(du, 0, 0, t, 1) for t in range(2)] + [(du, 0, 0, 2, k) for k in range(2)]
-        T += turns(("ds", 1, 0)) + [(du, 0, 0, 3, k) for k in range(2)] + [(du, 0, 0, t, 2) for t in range(4)] + turns(("ds", 1, 1)) + [(du, 0, 0, t, 3) for t in range(4)]
-        S += [(g_out, 0), (g_out, 1)] + pairs2(("ds", 0, 0)) + pairs2(("ds", 0, 1)) + wv(("z", 0, 1), 256) + pairs2(("ds", 0, 2)) + pairs2(("ds", 0, 3)) + pairs2(("ds", 1, 0)) + wv(("z", 0, 3), 512)
-        V += qq(("ds", 0, 0)) + wv(("z", 0, 0)) + qq(("ds", 0, 1)) + qq(("z", 0, 0)) + wv(("z", 0, 1), 0, 256) + qq(("z", 0, 1)) + qq(("ds", 0, 2)) + wv(("z", 0, 2)) + qq(("ds", 0, 3)) + qq(("z", 0, 2))
-        V += wv(("z", 0, 3), 0, 512) + qq(("ds", 1, 0)) + qq(("z", 0, 3)) + [(gain, 0, 0, t) for t in range(2)]
+        def D(h, t):
+            return ("ds", h, t)
 
-        S += pairs2(("ds", 1, 1)) + wv(("z", 1, 0)) + pairs2(("ds", 1, 2)) + wv(("z", 1, 1)) + pairs2(("ds", 1, 3)) + wv(("z", 1, 2)) + wv(("z", 1, 3), 256) + pairs2(("dp", 0, 0))
-        V += ge(0) + qq(("ds", 1, 1)) + ge(1) + ge(2) + qq(("z", 1, 0)) + ge(3) + qq(("ds", 1, 2)) + ge(4) + qq(("z", 1, 1)) + ge(5) + qq(("ds", 1, 3)) + ge(6) + wv(("z", 1, 3), 0, 256) + qq(("z", 1, 2)) + ge(7) + qq(("z", 1, 3))
-        T += tl(4) + turns(("ds", 1, 2)) + tl(5) + turns(("ds", 1, 3)) + tl(6) + [(du, 0, 1, t, k) for k in range(2) for t in range(2)] + tl(7) + turns(("dp", 0, 0))
-        T += [(du, 0, 1, t, 2) for t in range(2)] + [(du, 0, 1, 2, k) for k in range(3)] + [(du, 0, 1, t, 3) for t in range(3)] + tl(11)
-        S += wv(("z", 2, 0)) + wv(("z", 2, 1)) + pairs2(("dp", 1, 0)) + wv(("z", 2, 2)) + wv(("z", 2, 3)) + pairs2(("dp", 0, 1)) + pairs2(("m", 0))
-        V += ge(8) + qq(("dp", 0, 0)) + ge(9) + qq(("z", 2, 0)) + ge(10) + qq(("z", 2, 1)) + ge(11) + ge(12) + qq(("z", 2, 2)) + ge(13) + qq(("dp", 1, 0)) + ge(14) + qq(("z", 2, 3)) + ge(15)
-        T += tl(12) + turns(("dp", 1, 0)) + tl(13) + tl(14) + turns(("dp", 0, 1)) + tl(15) + [(du, 0, 2, t, k) for k in range(2) for t in range(2)] + turns(("m", 0)) + [(du, 0, 2, t, 2) for t in range(2)] + turns(("m", 1))
-        T += [(du, 0, 2, t, 3) for t in range(2)] + tl(18) + turns(("dp", 1, 1)) + tl(19) + turns(("m", 2)) + tl(20) + tl(21) + turns(("dp", 0, 2)) + tl(22) + tl(23)
-        S += pairs2(("m", 1)) + wv(wdp(0, 0)) + pairs2(("dp", 1, 1)) + pairs2(("m", 2)) + wv(("x", 0)) + pairs2(("dp", 0, 2)) + wv(("x", 1))
-        V += qq(("dp", 0, 1)) + ge(16) + qq(("m", 0)) + ge(17) + qq(("m", 1)) + ge(18) + ge(19) + qq(("dp", 1, 1)) + ge(20) + qq(("m", 2)) + ge(21) + qq(wdp(0, 0)) + ge(22) + qq(("dp", 0, 2)) + ge(23)
-        T += dxs(0, range(2)) + turns(("dp", 1, 2)) + dxs(0, range(2, 4)) + dms(0) + dxs(1) + dms(1) + dms(2)
-        V += wv(wdp(1, 0)) + qq(("x", 0)) + qq(wdp(1, 0)) + qq(("x", 1)) + qq(("dp", 1, 2)) + wv(wdp(0, 1)) + wv(wdp(1, 1)) + qq(wdp(0, 1)) + qq(wdp(1, 1))
-        V += wv(wdp(0, 2)) + wv(wdp(1, 2)) + qq(wdp(0, 2)) + qq(wdp(1, 2))
-        S += pairs2(("dp", 1, 2)) + [(out, "dx", 0, t) for t in range(4)] + [(out, "dm", 0, t) for t in range(4)] + [(out, "dx", 1, t) for t in range(4)] + [(out, "dm", 1, t) for t in range(4)]
+        def DP(h, q):
+            return ("dp", h, q)
+
+        T += turns(D(0, 0)) + [(spread, 0), (spread, 1)] + turns(D(0, 1))
+        T += [(du, 0, 0, 0, k) for k in range(2)] + turns(D(0, 2)) + [(du, 0, 0, 1, k) for k in range(2)] + turns(D(0, 3)) + [(du, 0, 0, t, 2) for t in range(2)]
+        T += [(du, 0, 0, 2, k) for k in range(3)] + [(du, 0, 0, t, 3) for t in range(3)]
+        HV = 320
+        for k in range(4):
+            V += wv(Z(0, k), 0, HV) + (qq(D(0, k - 1)) if k else []) + qq(Z(0, k))
+            S += wv(Z(0, k), HV) + pairs2(D(0, k))
+            if k == 0:
+                S += [(g_out, 0), (g_out, 1)]
+        V += wv(Z(1, 0), 0, 128) + qq(D(0, 3)) + gn(0, 0, 2) + ev(0) + gn(0, 2, 4)
+        T += turns(D(1, 0)) + tl(3) + turns(D(1, 1)) + tl(4) + turns(D(1, 2)) + tl(5) + turns(D(1, 3)) + tl(6) + [(du, 0, 1, t, k) for k in range(2) for t in range(2)] + turns(DP(0, 0)) + tl(7)
+        T += [(du, 0, 1, t, k) for k in range(2, 4) for t in range(2)] + tl(10) + tl(11)
+        S += wv(Z(1, 0), 128) + pairs2(D(1, 0)) + pairs2(D(1, 1)) + wv(Z(1, 1)) + pairs2(D(1, 2)) + pairs2(D(1, 3)) + wv(Z(1, 2)) + wv(Z(1, 3), 256) + pairs2(DP(0, 0))
+        V += ev(1) + qq(D(1, 0)) + ev(2, 3) + qq(D(1, 1)) + gn(1, 0, 2) + qq(Z(1, 0), Z(1, 1)) + qq(D(1, 2)) + ev(4) + qq(D(1, 3)) + ev(5) + gn(1, 2, 4) + wv(Z(1, 3), 0, 256) + ev(6) + qq(Z(1, 2), Z(1, 3)) + ev(7) + gn(2)
+        S += wv(Z(2, 0)) + wv(Z(2, 1)) + wv(Z(2, 2)) + wv(Z(2, 3)) + pairs2(DP(1, 0)) + pairs2(DP(0, 1)) + pairs2(("m", 0))
+        V += ev(8, 9) + gn(3, 0, 2) + ev(10) + qq(Z(2, 0), Z(2, 1)) + ev(11) + gn(3, 2, 4) + ev(12, 13) + qq(Z(2, 2), Z(2, 3)) + ev(14) + gn(4, 0, 2) + ev(15) + qq(DP(0, 0), DP(1, 0)) + gn(4, 2, 4)
+        T += tl(12) + tl(13) + turns(DP(1, 0)) + tl(14) + tl(15) + turns(DP(0, 1)) + [(du, 0, 2, t, k) for k in range(2) for t in range(2)] + turns(("m", 0))
+        T += [(du, 0, 2, t, k) for k in range(2, 4) for t in range(2)] + turns(("m", 1)) + tl(18) + turns(DP(1, 1)) + tl(19) + turns(("m", 2)) + tl(20) + turns(DP(0, 2)) + tl(21) + tl(22) + tl(23)
+        S += wv(wdp(0, 0)) + pairs2(("m", 1)) + pairs2(DP(1, 1)) + pairs2(("m", 2)) + wv(wdp(1, 0)) + pairs2(DP(0, 2)) + wv(("x", 0))
+        V += ev(16, 17) + gn(5, 0, 2) + ev(18, 19) + qq(("m", 0), ("m", 1)) + gn(5, 2, 4) + qq(DP(0, 1), DP(1, 1)) + ev(20) + qq(("m", 2)) + qq(DP(0, 2)) + ev(21, 22, 23) + qq(wdp(0, 0), wdp(1, 0))
+        T += dxs(0, range(2)) + turns(DP(1, 2)) + dxs(0, range(2, 4)) + dxs(1) + dms(0) + dms(1) + dms(2)
+        V += wv(("x", 1), 0, 256) + qq(DP(1, 2)) + wv(wdp(0, 1)) + qq(("x", 0), ("x", 1)) + wv(wdp(1, 1)) + wv(wdp(0, 2), 0, 512) + qq(wdp(0, 1), wdp(1, 1)) + wv(wdp(1, 2)) + qq(wdp(0, 2)) + qq(wdp(1, 2))
+        S += [(out, "dx", 0, 0)] + pairs2(DP(1, 2)) + [(out, "dx", 0, 1)] + wv(("x", 1), 256) + [(out, "dx", 0, t) for t in range(2, 4)] + [(out, "dx", 1, t) for t in range(4)] + wv(wdp(0, 2), 512) + [(out, "dm", 0, t) for t in range(4)] + [(out, "dm", 1, t) for t in range(4)]
         for t in range(4):
             (S if t % 2 else V).append((out, "dm", 2, t))
 

from contextlib import ExitStack

import concourse.mybir as mybir
from concourse.masks import make_identity

A, B, F, C = 1024, 2048, 1536, 512
FLOPS = 2 * A * B * F + 4 * A * F * C

F32 = mybir.dt.float32
BF16 = mybir.dt.bfloat16
U32 = mybir.dt.uint32
U8 = mybir.dt.uint8
E4M3 = mybir.dt.float8_e4m3fn_x4
E5M2 = mybir.dt.float8_e5m2_x4
MULT = mybir.AluOpType.mult

P = 128
W = 512


def tile_pair_score_metric_backward_s6_kernel(tc, ds, z, d, g, metric, x, out_0, out_1):
    nc = tc.nc
    with ExitStack() as ctx:
        sb = ctx.enter_context(tc.tile_pool(name="sb", bufs=1))
        ps = ctx.enter_context(tc.psum_pool(name="ps", bufs=1))
        ctx.enter_context(tc.manual_schedule())

        def tiles(name, count, width, dtype):
            return [sb.tile([P, width], dtype, name="%s%d" % (name, i), align_bytes=64) for i in range(count)]

        def operands(name, count):
            return list(zip(tiles(name + "c", count, 2 * W, U32), tiles(name + "s", count, 2 * W, U8)))

        free = {
            "bank": [ps.tile([P, W], F32, name="bank%d" % i) for i in range(8)],
            "raw": tiles("raw", 16, 4 * W, BF16),
            "grp": tiles("grp", 5, 8 * W, BF16),
            "gd": tiles("gd", 2, 4 * W, F32),
            "dp": tiles("dp", 6, 4 * W, BF16),
            "res": tiles("res", 8, W, F32),
            "e4": operands("e4", 5),
            "e5": operands("e5", 8),
        }
        ident = tiles("ident", 1, P, F32)[0]
        g_words = tiles("gw", 1, 6, F32)[0]
        g_all = tiles("gall", 1, F, BF16)[0]
        nc.scalar.dma_start(
            out=g_words[:].rearrange("p (a c) -> p a c", a=2),
            in_=g.bitcast(F32).rearrange("(a p c) -> p a c", a=2, c=3),
        )
        make_identity(nc, ident[:])

        have = {}
        done = set()
        left = {}

        def take(kind, key, uses):
            have[key] = free[kind].pop(0)
            left[key] = [kind, uses]
            return have[key]

        def used(key, amount=1):
            left[key][1] -= amount
            if left[key][1] == 0:
                kind = left.pop(key)[0]
                free[kind].append(have.pop(key))
                if kind == "raw":
                    load_more()

        def rows4(src):
            return src.rearrange("(p j) w -> p j w", j=4)

        def blk(i):
            return slice(i * W, (i + 1) * W)

        def source(key):
            if key[0] == "x":
                return rows4(x[blk(key[1]), :]), W
            if key[0] == "ds":
                return rows4(ds[blk(key[1]), :])[:, key[2], :].rearrange("p (j w) -> p j w", j=4), 2
            if key[0] == "d":
                return rows4(d[blk(key[1]), blk(key[2])]), 4
            if key[0] == "m":
                return metric[:, blk(key[1])].rearrange("(j p) w -> p j w", j=4), 2
            return rows4(z[blk(key[2]), blk(key[1])]), W

        order = [key for k in range(4) for key in (("z", 0, k), ("ds", 0, k))] + [("z", 1, 0), ("d", 0, 0), ("ds", 1, 0), ("ds", 1, 1), ("z", 1, 1), ("ds", 1, 2), ("d", 1, 0), ("ds", 1, 3), ("z", 1, 2), ("z", 1, 3), ("d", 0, 1), ("z", 2, 0), ("d", 1, 1)] + [("z", 2, k) for k in range(1, 4)] + [("d", 0, 2), ("m", 0), ("m", 1), ("d", 1, 2), ("m", 2), ("x", 0), ("x", 1)]

        def load_more():
            while order and free["raw"]:
                key = order.pop(0)
                src, uses = source(key)
                tile = take("raw", ("in",) + key, uses)
                nc.sync.dma_start(out=tile[:].rearrange("p (j w) -> p j w", j=4), in_=src)
                done.add(("in",) + key)

        def copy(eng, out, in_):
            if eng == "V":
                nc.vector.tensor_copy(out=out, in_=in_)
            else:
                nc.scalar.copy(out=out, in_=in_)

        def obtain(kind, key, uses):
            if key not in have:
                if not free[kind]:
                    return None
                take(kind, key, uses)
            return have[key]

        def filled(key, amount, total):
            left["fill", key] = left.get(("fill", key), 0) + amount
            if left["fill", key] == total:
                done.add(key)

        def pair_of(key):
            if key[0] in ("dp", "w"):
                return key[:-2] + key[-1:], key[-2], 2
            if key == ("m", 2):
                return ("m", 1), 0, 1
            return key[:-1] + (key[-1] // 2,), key[-1] % 2, 2

        def staging(key):
            pair, side, count = pair_of(key)
            tile = obtain("grp", ("stage",) + pair, count)
            return None if tile is None else tile[:, side * 4 * W : (side + 1) * 4 * W]

        def weave(eng, key, lo, hi):
            src = ("in",) + key[1:] if key[0] == "w" else ("in",) + key
            if src not in done:
                return False
            dst = staging(key)
            if dst is None:
                return False
            rows = have[src][:].rearrange("p (t c i) -> p c t i", t=4, i=4)
            side = dst.rearrange("p (c i t) -> p c t i", t=4, i=4)
            copy(eng, side[:, lo // 4 : hi // 4], rows[:, lo // 4 : hi // 4])
            used(src, hi - lo)
            filled(("grp",) + key, hi - lo, W)
            return True

        uses_of = {"z": 8, "ds": 12, "m": 8, "x": 12, "dp": 4, "w": 4}

        def quant(eng, *keys):
            kind = "e4" if keys[0][0] in ("z", "m", "x") else "e5"
            if any(("grp",) + key not in done for key in keys):
                return False
            pair, side, count = pair_of(keys[0])
            operand = obtain(kind, ("q",) + pair, count * uses_of[pair[0]])
            if operand is None:
                return False
            cols = slice(side * W, (side + len(keys)) * W)
            nc.vector.quantize_mx(
                out=operand[0][:, cols].bitcast(E4M3 if kind == "e4" else E5M2),
                scales=operand[1][:, cols],
                in_=have[("stage",) + pair][:, side * 4 * W : (side + len(keys)) * 4 * W],
            )
            used(("stage",) + pair, len(keys))
            for key in keys:
                done.add(("q",) + key)
            return True

        def turn(eng, key, half):
            src = ("in",) + key
            need = ("part", half) + key if key[0] == "dp" else src
            if need not in done or not free["bank"]:
                return False
            bank = take("bank", ("t", half) + key, 1)
            words = have[src][:].bitcast(F32)
            for j in range(2):
                first = 256 * (2 * half + j)
                for u in range(2):
                    if key[0] == "dp":
                        part = words[:, first + P * u : first + P * (u + 1)]
                    else:
                        part = words[:, first + u : first + 256 : 2]
                    nc.tensor.transpose(bank[:, (2 * j + u) * P : (2 * j + u + 1) * P], part, ident[:])
            used(src)
            done.add(("t", half) + key)
            return True

        def pairs(eng, key, half):
            if ("t", half) + key not in done:
                return False
            dst = staging(key)
            if dst is None:
                return False
            copy(
                eng,
                dst.bitcast(F32)[:, blk(half)].rearrange("p (j r u) -> p j r u", j=2, u=2),
                have[("t", half) + key][:].rearrange("p (j u r) -> p j r u", j=2, u=2),
            )
            used(("t", half) + key)
            filled(("grp",) + key, 1, 2)
            return True

        def mm(acc, still, col, moving, step, steps):
            if ("q",) + still not in done or ("q",) + moving not in done:
                return False
            bank = obtain("bank", acc, 1)
            if bank is None:
                return False
            (pa, sa), (pb, sm) = pair_of(still)[:2], pair_of(moving)[:2]
            cols = slice(sa * W + col * P, sa * W + (col + 1) * P)
            a, b = have[("q",) + pa], have[("q",) + pb]
            nc.tensor.matmul_mx(
                out=bank[:],
                lhsT=a[0][:, cols].bitcast(E4M3 if still[0] == "x" else E5M2),
                lhsT_scale=a[1][:, cols],
                rhs=b[0][:, blk(sm)].bitcast(E5M2 if still[0] == "x" else E4M3),
                rhs_scale=b[1][:, blk(sm)],
                start=step == 0,
                stop=step == steps - 1,
            )
            used(("q",) + pa)
            used(("q",) + pb)
            filled(acc, 1, steps)
            return True

        def du(eng, h, q, t, k):
            return mm(("du", h, q, t), ("ds", h, t), k, ("z", q, k), k, 4)

        def dm(eng, q, c, h):
            return mm(("dm", q, c), ("x", h), c, ("w", "dp", h, q), h, 2)

        def dx(eng, h, t, q):
            return mm(("dx", h, t), ("dp", h, q), t, ("m", q), q, 3)

        def spread(eng, part):
            if not free["bank"]:
                return False
            bank = take("bank", ("g", part), 1)
            for c in range(3):
                col = 3 * part + c
                nc.tensor.transpose(bank[:, c * P : (c + 1) * P], g_words[:, col : col + 1].to_broadcast([P, P]), ident[:])
            done.add(("g", part))
            return True

        def g_out(eng, part):
            if ("g", part) not in done:
                return False
            words = g_all[:].bitcast(F32).rearrange("p (a n c) -> p a n c", a=2, c=3)
            copy(eng, words[:, part], have["g", part][:, : 3 * P].rearrange("p (c n) -> p n c", c=3))
            used(("g", part))
            filled("gall", 1, 2)
            return True

        def gain(eng, h, q, t0, t1):
            if ("in", "d", h, q) not in done or "gall" not in done:
                return False
            tile = obtain("gd", ("gd", h, q), 4)
            if tile is None:
                return False
            nc.vector.tensor_tensor(
                out=tile[:].rearrange("p (t f) -> p t f", t=4)[:, t0:t1],
                in0=have["in", "d", h, q][:].rearrange("p (t f) -> p t f", t=4)[:, t0:t1],
                in1=g_all[:, blk(q)].unsqueeze(1).to_broadcast([P, t1 - t0, W]),
                op=MULT,
            )
            used(("in", "d", h, q), t1 - t0)
            for t in range(t0, t1):
                done.add(("gd", h, q, t))
            return True

        def evac(eng, h, q, t):
            if ("du", h, q, t) not in done or ("gd", h, q, t) not in done:
                return False
            dst = obtain("dp", ("in", "dp", h, q), 2 + W)
            if dst is None:
                return False
            nc.vector.tensor_tensor(
                out=dst[:, blk(t)].rearrange("p (u m e) -> p u m e", u=2, e=2),
                in0=have["du", h, q, t][:].rearrange("p (m u e) -> p u m e", u=2, e=2),
                in1=have["gd", h, q][:, blk(t)].rearrange("p (m u e) -> p u m e", u=2, e=2),
                op=MULT,
            )
            used(("du", h, q, t))
            used(("gd", h, q))
            filled(("part", t // 2, "dp", h, q), 1, 2)
            filled(("in", "dp", h, q), 1, 4)
            return True

        def out(eng, kind, i, j):
            if (kind, i, j) not in done or not free["res"]:
                return False
            res = take("res", ("res", kind, i, j), 1)
            bank = have[kind, i, j]
            if kind == "dm":
                copy(eng, res[:].rearrange("p (m u e) -> p m u e", u=2, e=2), bank[:].rearrange("p (u m e) -> p m u e", u=2, e=2))
            else:
                copy(eng, res[:], bank[:])
            used((kind, i, j))
            done.add(("res", kind, i, j))
            return True

        def store(eng, kind, i, j):
            if ("res", kind, i, j) not in done:
                return False
            dst = out_1[j * P : (j + 1) * P, blk(i)] if kind == "dm" else rows4(out_0[blk(i), :])[:, j, :]
            nc.sync.dma_start(out=dst, in_=have["res", kind, i, j][:])
            used(("res", kind, i, j))
            return True

        def warm_prep(eng):
            zeros = take("grp", "zeros", 1)
            nc.vector.memset(zeros[:, : 4 * W].bitcast(U32), 0)
            a = take("e5", "warm5", 1)
            b = take("e4", "warm4", 1)
            take("bank", "warm", 1)
            nc.vector.quantize_mx(out=a[0][:, :P].bitcast(E5M2), scales=a[1][:, :P], in_=zeros[:, :W])
            nc.vector.quantize_mx(out=b[0][:, :W].bitcast(E4M3), scales=b[1][:, :W], in_=zeros[:, : 4 * W])
            used("zeros")
            done.add("warm")
            return True

        def warm(eng, count, last):
            if "warm" not in done:
                return False
            a, b = have["warm5"], have["warm4"]
            for i in range(count):
                nc.tensor.matmul_mx(
                    out=have["warm"][:],
                    lhsT=a[0][:, :P].bitcast(E5M2),
                    lhsT_scale=a[1][:, :P],
                    rhs=b[0][:, :W].bitcast(E4M3),
                    rhs_scale=b[1][:, :W],
                    start=True,
                    stop=True,
                )
            if last:
                used("warm5")
                used("warm4")
                used("warm")
            return True

        V, S, T, G = [], [], [], []
        def turns(key):
            return [(turn, key, 0), (turn, key, 1)]

        def pairs2(key):
            return [(pairs, key, 0), (pairs, key, 1)]

        def tile4(h, q, t):
            return [(du, h, q, t, k) for k in range(4)]

        def wv(key, lo=0, hi=W):
            return [(weave, key, lo, hi)] if lo < hi else []

        def qq(*keys):
            return [(quant,) + keys]

        def wdp(h, q):
            return ("w", "dp", h, q)

        units = [(h, q) for q in range(3) for h in range(2)]

        def ev(*ns):
            return [(evac,) + units[n // 4] + (n % 4,) for n in ns]

        def gn(u, t0=0, t1=4):
            return [(gain,) + units[u] + (t0, t1)]

        def tl(n):
            return tile4(*units[n // 4], n % 4)

        def dxs(h, ts=range(4)):
            return [(dx, h, t, q) for t in ts for q in range(3)]

        def dms(q, cs=range(4)):
            return [(dm, q, c, h) for c in cs for h in range(2)]

        def Z(q, k):
            return ("z", q, k)

        def D(h, t):
            return ("ds", h, t)

        def DP(h, q):
            return ("dp", h, q)

        T += turns(D(0, 0)) + [(spread, 0), (spread, 1)] + turns(D(0, 1))
        T += [(du, 0, 0, 0, k) for k in range(2)] + turns(D(0, 2)) + [(du, 0, 0, 1, k) for k in range(2)] + turns(D(0, 3)) + [(du, 0, 0, t, 2) for t in range(2)]
        T += [(du, 0, 0, 2, k) for k in range(3)] + [(du, 0, 0, t, 3) for t in range(3)]
        HV = 320
        for k in range(4):
            V += wv(Z(0, k), 0, HV) + (qq(D(0, k - 1)) if k else []) + qq(Z(0, k))
            S += wv(Z(0, k), HV) + pairs2(D(0, k))
            if k == 0:
                S += [(g_out, 0), (g_out, 1)]
        V += wv(Z(1, 0), 0, 128) + qq(D(0, 3)) + gn(0, 0, 2) + ev(0) + gn(0, 2, 4)
        T += turns(D(1, 0)) + tl(3) + turns(D(1, 1)) + tl(4) + turns(D(1, 2)) + tl(5) + turns(D(1, 3)) + tl(6) + [(du, 0, 1, t, k) for k in range(2) for t in range(2)] + turns(DP(0, 0)) + tl(7)
        T += [(du, 0, 1, t, k) for k in range(2, 4) for t in range(2)] + tl(10) + tl(11)
        S += wv(Z(1, 0), 128) + pairs2(D(1, 0)) + pairs2(D(1, 1)) + wv(Z(1, 1)) + pairs2(D(1, 2)) + pairs2(D(1, 3)) + wv(Z(1, 2)) + wv(Z(1, 3), 256) + pairs2(DP(0, 0))
        V += ev(1) + qq(D(1, 0)) + ev(2, 3) + qq(D(1, 1)) + gn(1, 0, 2) + qq(Z(1, 0), Z(1, 1)) + qq(D(1, 2)) + ev(4) + qq(D(1, 3)) + ev(5) + gn(1, 2, 4) + wv(Z(1, 3), 0, 256) + ev(6) + qq(Z(1, 2), Z(1, 3)) + ev(7) + gn(2)
        S += wv(Z(2, 0)) + wv(Z(2, 1)) + wv(Z(2, 2)) + wv(Z(2, 3)) + pairs2(DP(1, 0)) + pairs2(DP(0, 1)) + pairs2(("m", 0))
        V += ev(8, 9) + gn(3, 0, 2) + ev(10) + qq(Z(2, 0), Z(2, 1)) + ev(11) + gn(3, 2, 4) + ev(12, 13) + qq(Z(2, 2), Z(2, 3)) + ev(14) + gn(4, 0, 2) + ev(15) + qq(DP(0, 0), DP(1, 0)) + gn(4, 2, 4)
        T += tl(12) + tl(13) + turns(DP(1, 0)) + tl(14) + tl(15) + turns(DP(0, 1)) + [(du, 0, 2, t, k) for k in range(2) for t in range(2)] + turns(("m", 0))
        T += [(du, 0, 2, t, k) for k in range(2, 4) for t in range(2)] + turns(("m", 1)) + tl(18) + turns(DP(1, 1)) + tl(19) + turns(("m", 2)) + tl(20) + turns(DP(0, 2)) + tl(21) + tl(22) + tl(23)
        S += wv(wdp(0, 0)) + pairs2(("m", 1)) + pairs2(DP(1, 1)) + pairs2(("m", 2)) + wv(wdp(1, 0)) + pairs2(DP(0, 2)) + wv(("x", 0))
        V += ev(16, 17) + gn(5, 0, 2) + ev(18, 19) + qq(("m", 0), ("m", 1)) + gn(5, 2, 4) + qq(DP(0, 1), DP(1, 1)) + ev(20) + qq(("m", 2)) + qq(DP(0, 2)) + ev(21, 22, 23) + qq(wdp(0, 0), wdp(1, 0))
        T += dxs(0, range(2)) + turns(DP(1, 2)) + dxs(0, range(2, 4)) + dxs(1) + dms(0) + dms(1) + dms(2)
        V += wv(("x", 1), 0, 256) + qq(DP(1, 2)) + wv(wdp(0, 1)) + qq(("x", 0), ("x", 1)) + wv(wdp(1, 1)) + wv(wdp(0, 2), 0, 512) + qq(wdp(0, 1), wdp(1, 1)) + wv(wdp(1, 2)) + qq(wdp(0, 2)) + qq(wdp(1, 2))
        S += [(out, "dx", 0, 0)] + pairs2(DP(1, 2)) + [(out, "dx", 0, 1)] + wv(("x", 1), 256) + [(out, "dx", 0, t) for t in range(2, 4)] + [(out, "dx", 1, t) for t in range(4)] + wv(wdp(0, 2), 512) + [(out, "dm", 0, t) for t in range(4)] + [(out, "dm", 1, t) for t in range(4)]
        for t in range(4):
            (S if t % 2 else V).append((out, "dm", 2, t))

        load_more()
        Y = [(store, "dm") + s[1:3] if s[0] is dm else (store, "dx") + s[1:3] for s in T if (s[0] is dm and s[3] == 1) or (s[0] is dx and s[3] == 2)]
        queues = {"V": V, "S": S, "T": T, "G": G, "Y": Y}
        while any(queues.values()):
            moved = False
            for eng, steps in queues.items():
                if steps and steps[0][0](eng, *steps[0][1:]):
                    steps.pop(0)
                    moved = True
            assert moved, str([s[0][1:] for s in queues.values() if s])
